import numpy as np
import ml_dtypes


def mxq(x, axis, fmt="e4m3"):
    dtype, down = {"e4m3": (ml_dtypes.float8_e4m3fn, 7), "e5m2": (ml_dtypes.float8_e5m2, 14)}[fmt]
    v = np.moveaxis(np.asarray(x, np.float32).astype(ml_dtypes.bfloat16).astype(np.float64), axis, -1)
    blocks = v.reshape(v.shape[:-1] + (-1, 32))
    amax = np.abs(blocks).max(-1, keepdims=True)
    byte = np.maximum(np.where(amax > 0, np.frexp(amax)[1] - 1 + 127, 0) - down, 1)
    scale = np.exp2(byte - 127.0)
    codes = (blocks / scale).astype(np.float32).astype(dtype).astype(np.float64)
    return np.moveaxis((codes * scale).reshape(v.shape), -1, axis)


WIDE = False


def mx_kscale(k):
    if not WIDE:
        return np.ones(k)
    levels = np.array([10, -10, 5, -5, 0])
    if k % 512:
        return np.exp2(np.random.permutation(np.resize(levels, k // 32))).repeat(32)
    a = np.empty((k // 512, 16))
    for p in range(k // 512):
        a[p, :8] = np.random.permutation(np.resize(levels, 8))
        for g in range(8):
            far = levels[np.abs(levels - a[p, g]) >= 10]
            a[p, g + 8] = far[np.random.randint(len(far))]
    return np.exp2(a.ravel()).repeat(32)


def f64(x):
    return np.asarray(x).astype(np.float64)


def striped(idx):
    return np.tile(idx.reshape(-1, 16).T, (8, 1)).astype(np.uint16)


def unstriped(offs):
    return offs[:16].T.reshape(-1).astype(np.int64)


def striped8(idx):
    return np.concatenate([x.reshape(-1, 16).T for x in idx]).astype(np.uint16)


def runs(offs, k):
    lists = np.stack([offs[16 * r : 16 * r + 16].T.reshape(-1) for r in range(8)]).astype(np.int64)
    return lists[np.arange(k) % 512 // 64]


def pack_weight(w):
    k, n = w.shape
    w = f64(np.asarray(w, np.float32).astype(ml_dtypes.bfloat16)).reshape(k // 32, 32, n)
    amax = np.abs(w).max(1)
    byte = np.clip(np.where(amax > 0, np.frexp(amax)[1] - 1 + 127 - 7, 1), 1, 254)
    scaled = (w * np.exp2(127.0 - byte)[:, None, :]).reshape(k, n).astype(np.float32)
    words = np.ascontiguousarray(scaled.reshape(k // 512, 128, 4, n).transpose(0, 1, 3, 2)).astype(ml_dtypes.float8_e4m3fn).view(np.uint8)
    return words, np.ascontiguousarray(byte.astype(np.uint8).reshape(k // 512, 16, n))


def unpack_weight(words, scales):
    g, p, n, _ = words.shape
    vals = np.ascontiguousarray(words).view(ml_dtypes.float8_e4m3fn).astype(np.float64) * np.repeat(np.exp2(scales.astype(np.float64) - 127.0), 8, axis=1)[..., None]
    return vals.transpose(0, 1, 3, 2).reshape(g * 512, n)


K, T, S, V, N, H = 512, 2048, 512, 256, 512, 512


def setup_inputs():
    n = np.random.standard_normal
    s = mx_kscale(K)[:, None]
    u = mx_kscale(H)
    packed_xT = pack_weight(n((K, T)) * s)
    perm = np.stack([np.random.permutation(S) for _ in range(8)])
    return {
        "x_words": packed_xT[0],
        "x_scales": packed_xT[1],
        "w1": (n((K, H)) / np.sqrt(K) / s * u).astype(np.float32),
        "w2": (n((H, H)) / np.sqrt(H) / u[:, None] * u).astype(np.float32),
        "res": (2 * n((N, S))).astype(np.float32),
        "w3": (n((H, N)) / np.sqrt(H) / u[:, None]).astype(np.float32),
        "offs": striped(np.random.permutation(T)[:S]),
        "la": striped8(perm[:, :V]),
        "lb": striped8(perm[:, V:]),
        "mate": striped8(np.stack([np.random.permutation(S) for _ in range(8)])),
    }


def reference(x_words, x_scales, w1, w2, res, w3, offs, la, lb, mate):
    xq = unpack_weight(x_words, x_scales)[:, unstriped(offs)]
    y = mxq(f64(w1), 0, "e4m3").T @ xq
    a = y[np.arange(H)[:, None], runs(la, H)]
    b = y[np.arange(H)[:, None], runs(lb, H)]
    mx = np.maximum(a, b)
    mn = np.minimum(a, b)
    p = np.zeros((H, S))
    p[np.arange(H)[:, None], runs(la, H)] = mn
    z = p.copy()
    z[np.arange(H)[:, None], runs(lb, H)] = mx
    h = mxq(f64(w2), 0, "e4m3").T @ mxq(z, 0, "e4m3")
    z2 = np.maximum(h, h[np.arange(H)[:, None], runs(mate, H)])
    return f64(res) + (mxq(f64(w3), 0, "e4m3").T @ mxq(z2, 0, "e4m3"))

@@ -1,0 +1,237 @@
+from contextlib import ExitStack
+
+import concourse.mybir as mybir
+
+K, T, S, V = 512, 2048, 512, 256
+FLOPS = 3 * 2 * K * K * S
+
+F32 = mybir.dt.float32
+BF16 = mybir.dt.bfloat16
+I32 = mybir.dt.int32
+U32 = mybir.dt.uint32
+U16 = mybir.dt.uint16
+U8 = mybir.dt.uint8
+FP8X4 = mybir.dt.float8_e4m3fn_x4
+ALU = mybir.AluOpType
+COPY = mybir.ActivationFunctionType.Copy
+
+P = 128
+PACK = 4
+HALF = S // 2
+QUARTER = S // 4
+PER_COLUMN = 16
+PLANE_ORDER = (0, 2, 3, 1)
+
+
+def tile_picked_sortlay_none_p_kernel(
+    tc, x_words, x_scales, w1, w2, res, w3, offs, la, lb, mate, out
+):
+    nc = tc.nc
+
+    with ExitStack() as ctx:
+        lists = ctx.enter_context(tc.tile_pool(name="lists", bufs=1))
+        keep = ctx.enter_context(tc.tile_pool(name="keep", bufs=1))
+        psum = ctx.enter_context(tc.psum_pool(name="psum", bufs=1))
+
+        def tile(name, shape, dtype, tag=None):
+            return keep.tile(shape, dtype, name=name, tag=tag or name, align_bytes=64)
+
+        def bank(name, shape, number):
+            return psum.tile(shape, F32, name=name, tag="bank%d" % number)
+
+        def load_list(name, source):
+            held = lists.tile(list(source.shape), U16, name=name)
+            nc.sync.dma_start(held[:], source)
+            return held
+
+        def load_weight(name, source):
+            raw = tile(name, [P, PACK, K], F32)
+            nc.sync.dma_start(raw[:], source.rearrange("(p j) c -> p j c", j=PACK))
+            return raw
+
+        def scalar_copy(dst, src):
+            nc.scalar.activation(dst, src, COPY)
+
+        def vector_copy(dst, src):
+            nc.vector.tensor_copy(dst, src)
+
+        def deal_half(copy, name, raw, u):
+            grouped = tile(name, [P, 2, P, PACK], BF16)
+            copy(
+                grouped[:].rearrange("p t m j -> p m j t"),
+                raw[:].rearrange("p j (m t) -> p m j t", t=PACK)[:, :, :, 2 * u : 2 * u + 2],
+            )
+            return grouped[:].rearrange("p t m j -> p (t m j)")
+
+        def quantize(name, grouped, tag=None):
+            width = grouped.shape[1] // PACK
+            codes = tile(name + "_codes", [P, width], U32, tag)
+            scales = tile(name + "_scales", [P, width], U8)
+            nc.vector.quantize_mx(out=codes[:].bitcast(FP8X4), scales=scales[:], in_=grouped)
+            return codes, scales
+
+        def product(acc, weights, weight_cols, tokens, token_cols):
+            nc.tensor.matmul_mx(
+                out=acc,
+                lhsT=weights[0][:, weight_cols].bitcast(FP8X4),
+                lhsT_scale=weights[1][:, weight_cols],
+                rhs=tokens[0][:, token_cols].bitcast(FP8X4),
+                rhs_scale=tokens[1],
+                start=True,
+                stop=True,
+            )
+
+        def cols(n, width):
+            return slice(n * width, (n + 1) * width)
+
+        x_bytes = tile("x_bytes", [P, T], U8)
+        nc.vector.memset(x_bytes[:].bitcast(I32), 0)
+        w1_raw = load_weight("w1_raw", w1)
+        for quadrant in range(4):
+            nc.sync.dma_start(
+                x_bytes[32 * quadrant : 32 * quadrant + 4, :].bitcast(I32),
+                x_scales[0, cols(quadrant, 4), :].bitcast(I32),
+            )
+        offs_list = load_list("offs_list", offs)
+        x_table = tile("x_table", [P, T], U32)
+        nc.sync.dma_start(x_table[:].bitcast(I32), x_words[0].rearrange("p n t -> p (n t)").bitcast(I32))
+        la_list = load_list("la_list", la)
+        lb_list = load_list("lb_list", lb)
+        w2_raw = load_weight("w2_raw", w2)
+        w3_raw = load_weight("w3_raw", w3)
+        mate_list = load_list("mate_list", mate)
+        res_rows = []
+        for q in range(4):
+            rows = tile("res_rows%d" % q, [P, PACK, QUARTER], F32)
+            nc.sync.dma_start(rows[:], res.rearrange("(m p) c -> p m c", p=P)[:, :, cols(q, QUARTER)])
+            res_rows.append(rows)
+
+        picked_bytes = tile("picked_bytes", [P, S], U8)
+        nc.vector.tensor_copy(picked_bytes[:], x_bytes[:].indirect(offs_list[:]))
+        w1_grouped = [deal_half(vector_copy, "w1_grouped0", w1_raw, 0), deal_half(scalar_copy, "w1_grouped1", w1_raw, 1)]
+        w1_mx = [quantize("w1_%d" % u, w1_grouped[u]) for u in range(2)]
+        picked_words = []
+        for half in range(2):
+            words = tile("picked_words%d" % half, [P, HALF], U32)
+            nc.vector.tensor_copy(words[:], x_table[:].indirect(offs_list[:, cols(half, HALF // PER_COLUMN)]))
+            picked_words.append(words)
+
+        y_banks = {}
+        for t in PLANE_ORDER:
+            for half in range(2):
+                acc = bank("y_bank%d_%d" % (t, half), [P, HALF], 2 * t + half)
+                product(acc[:], w1_mx[t // 2], cols(t % 2, P), (picked_words[half], picked_bytes[:, cols(half, HALF)]), slice(0, HALF))
+                y_banks[t, half] = acc
+
+        pairs = {}
+        for t in PLANE_ORDER:
+            second = vector_copy if t == PLANE_ORDER[0] else scalar_copy
+            y_row = tile("y_row%d" % t, [P, S], F32)
+            scalar_copy(y_row[:, cols(0, HALF)], y_banks[t, 0][:])
+            second(y_row[:, cols(1, HALF)], y_banks[t, 1][:])
+            at_la = tile("at_la%d" % t, [P, V], F32)
+            at_lb = tile("at_lb%d" % t, [P, V], F32)
+            scalar_copy(at_la[:], y_row[:].indirect(la_list[:]))
+            second(at_lb[:], y_row[:].indirect(lb_list[:]))
+            pairs[t] = (at_la, at_lb)
+
+        w2_grouped = [deal_half(scalar_copy, "w2_grouped%d" % u, w2_raw, u) for u in range(2)]
+
+        z_grouped = [tile("z_grouped%d" % half, [P, HALF, PACK], BF16) for half in range(2)]
+
+        def group_w3(half):
+            grouped = tile("w3_grouped%d" % half, [P, HALF, PACK], BF16)
+            scalar_copy(
+                grouped[:].rearrange("p (c i) j -> p c j i", i=4),
+                w3_raw[:, :, cols(half, HALF)].rearrange("p j (c i) -> p c j i", i=4),
+            )
+            return grouped[:].rearrange("p c j -> p (c j)")
+
+        w3_grouped = []
+
+        w2_mx = []
+        for t in PLANE_ORDER:
+            last = t == PLANE_ORDER[-1]
+            smaller = tile("smaller%d" % t, [P, V], F32)
+            larger = tile("larger%d" % t, [P, V], F32)
+            nc.vector.tensor_tensor(smaller[:], pairs[t][0][:], pairs[t][1][:], ALU.min)
+            nc.vector.tensor_tensor(larger[:], pairs[t][0][:], pairs[t][1][:], ALU.max)
+            if last:
+                w2_mx = [quantize("w2_%d" % u, w2_grouped[u]) for u in range(2)]
+            z_row = tile("z_row%d" % t, [P, S], F32, "z_row%d" % (0 if t < 2 else t))
+            nc.vector.tensor_copy(z_row[:].indirect(la_list[:]), smaller[:])
+            nc.vector.tensor_copy(z_row[:].indirect(lb_list[:]), larger[:])
+            if t == PLANE_ORDER[2]:
+                w3_grouped.append(group_w3(0))
+            first = vector_copy if last else scalar_copy
+            first(z_grouped[0][:, :, t], z_row[:, cols(0, HALF)])
+            scalar_copy(z_grouped[1][:, :, t], z_row[:, cols(1, HALF)])
+
+        z_mx = [quantize("z_%d" % half, z_grouped[half][:].rearrange("p c t -> p (c t)")) for half in range(2)]
+        w3_mx = [quantize("w3_0", w3_grouped[0], "z_row0")]
+        w3_grouped.append(group_w3(1))
+
+        h_rows = [tile("h_row%d" % t, [P, S], F32) for t in range(PACK)]
+        h_banks = []
+        for q in range(4):
+            acc = bank("h_bank%d" % q, [P, PACK, QUARTER], q)
+            codes, scales = z_mx[q // 2]
+            for t in range(PACK):
+                product(acc[:, t, :], w2_mx[t // 2], cols(t % 2, P), (codes, scales[:, cols(q % 2, QUARTER)]), cols(q % 2, QUARTER))
+            h_banks.append(acc)
+        for q in range(4):
+            copy = vector_copy if q % 2 else scalar_copy
+            for t in range(PACK):
+                copy(h_rows[t][:, cols(q, QUARTER)], h_banks[q][:, t, :])
+            if q == 1:
+                w3_mx.append(quantize("w3_1", w3_grouped[1]))
+
+        out_rows = out.rearrange("(m p) c -> p m c", p=P)
+        at_mate, z2_grouped, out_banks = {}, {}, {}
+
+        def fetch_mates(q):
+            at_mate[q] = tile("at_mate%d" % q, [P, PACK, QUARTER], F32)
+            for t in range(PACK):
+                copy = vector_copy if q == 0 and t >= 2 else scalar_copy
+                copy(at_mate[q][:, t, :], h_rows[t][:].indirect(mate_list[:, cols(q, QUARTER // PER_COLUMN)]))
+
+        def compete(q):
+            tag = ("z2_grouped0", "z2_grouped1", "z2_grouped0", "res_rows0")[q]
+            z2_grouped[q] = tile("z2_grouped%d" % q, [P, QUARTER, PACK], BF16, tag)
+            nc.vector.tensor_tensor(
+                z2_grouped[q][:],
+                h_banks[q][:].rearrange("p t c -> p c t"),
+                at_mate[q][:].rearrange("p t c -> p c t"),
+                ALU.max,
+            )
+
+        def last_product(q):
+            codes, scales = quantize("z2_%d" % q, z2_grouped[q][:].rearrange("p c t -> p (c t)"))
+            pieces = [(0, 2, 7), (2, 2, 0)] if q == 3 else [(0, 4, 4 + q)]
+            out_banks[q] = []
+            for first, count, number in pieces:
+                acc = bank("out_bank%d_%d" % (q, first), [P, count, QUARTER], number)
+                for m in range(first, first + count):
+                    product(acc[:, m - first, :], w3_mx[m // 2], cols(m % 2, P), (codes, scales[:]), slice(0, QUARTER))
+                out_banks[q].append((slice(first, first + count), acc))
+
+        def finish(q):
+            for blocks, acc in out_banks[q]:
+                result = tile("result%d_%d" % (q, blocks.start), list(acc.shape), F32)
+                nc.vector.tensor_tensor(result[:], acc[:], res_rows[q][:, blocks, :], ALU.add)
+                nc.sync.dma_start(out_rows[:, blocks, cols(q, QUARTER)], result[:])
+
+        for q in range(4):
+            fetch_mates(q)
+        compete(0)
+        compete(1)
+        last_product(0)
+        last_product(1)
+        compete(2)
+        finish(0)
+        last_product(2)
+        compete(3)
+        finish(1)
+        last_product(3)
+        finish(2)
+        finish(3)

@@ -20,7 +20,7 @@ PACK = 4
 HALF = S // 2
 QUARTER = S // 4
 PER_COLUMN = 16
-PLANE_ORDER = (0, 2, 3, 1)
+PLANE_ORDER = (2, 0, 1, 3)
 
 
 def tile_picked_sortlay_none_p_kernel(
@@ -84,15 +84,18 @@ def tile_picked_sortlay_none_p_kernel(
         def cols(n, width):
             return slice(n * width, (n + 1) * width)
 
+        def entries(held, piece):
+            return held[:, piece.start // PER_COLUMN : piece.stop // PER_COLUMN]
+
         x_bytes = tile("x_bytes", [P, T], U8)
         nc.vector.memset(x_bytes[:].bitcast(I32), 0)
+        offs_list = load_list("offs_list", offs)
         w1_raw = load_weight("w1_raw", w1)
         for quadrant in range(4):
             nc.sync.dma_start(
                 x_bytes[32 * quadrant : 32 * quadrant + 4, :].bitcast(I32),
                 x_scales[0, cols(quadrant, 4), :].bitcast(I32),
             )
-        offs_list = load_list("offs_list", offs)
         x_table = tile("x_table", [P, T], U32)
         nc.sync.dma_start(x_table[:].bitcast(I32), x_words[0].rearrange("p n t -> p (n t)").bitcast(I32))
         la_list = load_list("la_list", la)
@@ -108,36 +111,42 @@ def tile_picked_sortlay_none_p_kernel(
 
         picked_bytes = tile("picked_bytes", [P, S], U8)
         nc.vector.tensor_copy(picked_bytes[:], x_bytes[:].indirect(offs_list[:]))
-        w1_grouped = [deal_half(vector_copy, "w1_grouped0", w1_raw, 0), deal_half(scalar_copy, "w1_grouped1", w1_raw, 1)]
-        w1_mx = [quantize("w1_%d" % u, w1_grouped[u]) for u in range(2)]
-        picked_words = []
-        for half in range(2):
-            words = tile("picked_words%d" % half, [P, HALF], U32)
-            nc.vector.tensor_copy(words[:], x_table[:].indirect(offs_list[:, cols(half, HALF // PER_COLUMN)]))
-            picked_words.append(words)
+        w1_grouped = {1: deal_half(vector_copy, "w1_grouped1", w1_raw, 1), 0: deal_half(scalar_copy, "w1_grouped0", w1_raw, 0)}
+        w1_mx = {u: quantize("w1_%d" % u, w1_grouped[u]) for u in (1, 0)}
+        picked_words = tile("picked_words", [P, S], U32)
+        token_pieces = (slice(0, HALF), slice(HALF, HALF + QUARTER), slice(HALF + QUARTER, S))
+        for piece in token_pieces:
+            nc.vector.tensor_copy(picked_words[:, piece], x_table[:].indirect(entries(offs_list, piece)))
 
-        y_banks = {}
-        for t in PLANE_ORDER:
-            for half in range(2):
-                acc = bank("y_bank%d_%d" % (t, half), [P, HALF], 2 * t + half)
-                product(acc[:], w1_mx[t // 2], cols(t % 2, P), (picked_words[half], picked_bytes[:, cols(half, HALF)]), slice(0, HALF))
-                y_banks[t, half] = acc
+        first, last = PLANE_ORDER[0], PLANE_ORDER[-1]
+        y_pieces = [(first, piece) for piece in token_pieces] + [(t, slice(0, S)) for t in PLANE_ORDER[1:]]
+        y_banks = []
+        for number, (t, piece) in enumerate(y_pieces):
+            acc = bank("y_bank%d" % number, [P, piece.stop - piece.start], min(number, 2))
+            product(acc[:], w1_mx[t // 2], cols(t % 2, P), (picked_words, picked_bytes[:, piece]), piece)
+            y_banks.append(acc)
 
-        pairs = {}
+        at_la, at_lb, smaller, larger, z_rows = {}, {}, {}, {}, {}
+        pair_pieces = {t: (slice(0, V),) for t in PLANE_ORDER}
+        pair_pieces[first] = (slice(0, V // 2), slice(V // 2, V))
         for t in PLANE_ORDER:
-            second = vector_copy if t == PLANE_ORDER[0] else scalar_copy
             y_row = tile("y_row%d" % t, [P, S], F32)
-            scalar_copy(y_row[:, cols(0, HALF)], y_banks[t, 0][:])
-            second(y_row[:, cols(1, HALF)], y_banks[t, 1][:])
-            at_la = tile("at_la%d" % t, [P, V], F32)
-            at_lb = tile("at_lb%d" % t, [P, V], F32)
-            scalar_copy(at_la[:], y_row[:].indirect(la_list[:]))
-            second(at_lb[:], y_row[:].indirect(lb_list[:]))
-            pairs[t] = (at_la, at_lb)
+            for (plane, piece), acc in zip(y_pieces, y_banks):
+                if plane == t:
+                    scalar_copy(y_row[:, piece], acc[:])
+            at_la[t] = tile("at_la%d" % t, [P, V], F32)
+            at_lb[t] = tile("at_lb%d" % t, [P, V], F32)
+            for piece in pair_pieces[t]:
+                copy = vector_copy if t == first and piece.start == 0 else scalar_copy
+                scalar_copy(at_la[t][:, piece], y_row[:].indirect(entries(la_list, piece)))
+                copy(at_lb[t][:, piece], y_row[:].indirect(entries(lb_list, piece)))
 
-        w2_grouped = [deal_half(scalar_copy, "w2_grouped%d" % u, w2_raw, u) for u in range(2)]
+        w2_dealt = tile("w2_grouped", [P, PACK, P, PACK], BF16)
+        scalar_copy(w2_dealt[:].rearrange("p t m j -> p m j t"), w2_raw[:].rearrange("p j (m t) -> p m j t", t=PACK))
+        w2_grouped = [w2_dealt[:, 2 * u : 2 * u + 2].rearrange("p t m j -> p (t m j)") for u in range(2)]
 
-        z_grouped = [tile("z_grouped%d" % half, [P, HALF, PACK], BF16) for half in range(2)]
+        z_grouped = [tile("z_grouped%d" % q, [P, QUARTER, PACK], BF16) for q in range(4)]
+        z_pairs = tile("z_pairs", [P, 2, S - QUARTER, 2], BF16)
 
         def group_w3(half):
             grouped = tile("w3_grouped%d" % half, [P, HALF, PACK], BF16)
@@ -149,42 +158,67 @@ def tile_picked_sortlay_none_p_kernel(
 
         w3_grouped = []
 
-        w2_mx = []
         for t in PLANE_ORDER:
-            last = t == PLANE_ORDER[-1]
-            smaller = tile("smaller%d" % t, [P, V], F32)
-            larger = tile("larger%d" % t, [P, V], F32)
-            nc.vector.tensor_tensor(smaller[:], pairs[t][0][:], pairs[t][1][:], ALU.min)
-            nc.vector.tensor_tensor(larger[:], pairs[t][0][:], pairs[t][1][:], ALU.max)
-            if last:
-                w2_mx = [quantize("w2_%d" % u, w2_grouped[u]) for u in range(2)]
-            z_row = tile("z_row%d" % t, [P, S], F32, "z_row%d" % (0 if t < 2 else t))
-            nc.vector.tensor_copy(z_row[:].indirect(la_list[:]), smaller[:])
-            nc.vector.tensor_copy(z_row[:].indirect(lb_list[:]), larger[:])
+            smaller[t] = tile("smaller%d" % t, [P, V], F32)
+
+        def take_smaller(t, piece):
+            nc.vector.tensor_tensor(smaller[t][:, piece], at_la[t][:, piece], at_lb[t][:, piece], ALU.min)
+
+        def take_larger(t, tag):
+            larger[t] = tile("larger%d" % t, [P, V], F32, tag)
+            nc.vector.tensor_tensor(larger[t][:], at_la[t][:], at_lb[t][:], ALU.max)
+
+        def group_plane(t, copy_pairs):
+            scalar_copy(z_grouped[0][:, :, t], z_rows[t][:, 0:QUARTER])
+            copy_pairs(z_pairs[:, t // 2, :, t % 2], z_rows[t][:, QUARTER:S])
+
+        for t, following in zip(PLANE_ORDER, PLANE_ORDER[1:] + (None,)):
+            z_rows[t] = tile("z_row%d" % t, [P, S], F32, "z_row%d" % (first if t == last else t))
+            for piece in pair_pieces[t]:
+                if t == first:
+                    take_smaller(t, piece)
+                nc.vector.tensor_copy(z_rows[t][:].indirect(entries(la_list, piece)), smaller[t][:, piece])
+            take_larger(t, None if following is None else "y_row%d" % following)
+            if following is not None:
+                take_smaller(following, slice(0, V))
+            nc.vector.tensor_copy(z_rows[t][:].indirect(lb_list[:]), larger[t][:])
             if t == PLANE_ORDER[2]:
                 w3_grouped.append(group_w3(0))
-            first = vector_copy if last else scalar_copy
-            first(z_grouped[0][:, :, t], z_row[:, cols(0, HALF)])
-            scalar_copy(z_grouped[1][:, :, t], z_row[:, cols(1, HALF)])
-
-        z_mx = [quantize("z_%d" % half, z_grouped[half][:].rearrange("p c t -> p (c t)")) for half in range(2)]
-        w3_mx = [quantize("w3_0", w3_grouped[0], "z_row0")]
+            if following is not None:
+                group_plane(t, scalar_copy)
         w3_grouped.append(group_w3(1))
+        group_plane(last, vector_copy)
+        pair_words = z_pairs[:].rearrange("p u c e -> p u (c e)").bitcast(F32)
+        for q in range(1, 4):
+            nc.scalar.copy(
+                z_grouped[q][:].rearrange("p c t -> p (c t)").bitcast(F32).rearrange("p (c u) -> p c u", u=2),
+                pair_words[:, :, cols(q - 1, QUARTER)].rearrange("p u c -> p c u"),
+            )
 
-        h_rows = [tile("h_row%d" % t, [P, S], F32) for t in range(PACK)]
+        def quantize_z(q):
+            return quantize("z_%d" % q, z_grouped[q][:].rearrange("p c t -> p (c t)"))
+
+        w2_mx = [quantize("w2_0", w2_grouped[0], "smaller%d" % last)]
+        z_mx = [quantize_z(0)]
+        w2_mx.append(quantize("w2_1", w2_grouped[1], "larger%d" % last))
+        z_mx.extend(quantize_z(q) for q in range(1, 4))
+        w3_mx = [quantize("w3_0", w3_grouped[0], "z_row%d" % first)]
+
+        h_tags = ("z_grouped3", "z_grouped2", "z_pairs", "z_grouped1")
+        h_rows = [tile("h_row%d" % t, [P, S], F32, h_tags[t]) for t in range(PACK)]
         h_banks = []
         for q in range(4):
             acc = bank("h_bank%d" % q, [P, PACK, QUARTER], q)
-            codes, scales = z_mx[q // 2]
+            codes, scales = z_mx[q]
             for t in range(PACK):
-                product(acc[:, t, :], w2_mx[t // 2], cols(t % 2, P), (codes, scales[:, cols(q % 2, QUARTER)]), cols(q % 2, QUARTER))
+                product(acc[:, t, :], w2_mx[t // 2], cols(t % 2, P), (codes, scales[:]), slice(0, QUARTER))
             h_banks.append(acc)
         for q in range(4):
             copy = vector_copy if q % 2 else scalar_copy
             for t in range(PACK):
                 copy(h_rows[t][:, cols(q, QUARTER)], h_banks[q][:, t, :])
             if q == 1:
-                w3_mx.append(quantize("w3_1", w3_grouped[1]))
+                w3_mx.append(quantize("w3_1", w3_grouped[1], "z_grouped0"))
 
         out_rows = out.rearrange("(m p) c -> p m c", p=P)
         at_mate, z2_grouped, out_banks = {}, {}, {}

@@ -233,9 +233,9 @@ def tile_picked_sortlay_none_p_kernel(
             tag = ("z2_grouped0", "z2_grouped1", "z2_grouped0", "res_rows0")[q]
             z2_grouped[q] = tile("z2_grouped%d" % q, [P, QUARTER, PACK], BF16, tag)
             nc.vector.tensor_tensor(
-                z2_grouped[q][:],
-                h_banks[q][:].rearrange("p t c -> p c t"),
-                at_mate[q][:].rearrange("p t c -> p c t"),
+                z2_grouped[q][:].rearrange("p (c i) t -> p c t i", i=4),
+                h_banks[q][:].rearrange("p t (c i) -> p c t i", i=4),
+                at_mate[q][:].rearrange("p t (c i) -> p c t i", i=4),
                 ALU.max,
             )
 

@@ -126,7 +126,14 @@ def tile_picked_sortlay_none_p_kernel(
             product(acc[:], w1_mx[t // 2], cols(t % 2, P), (picked_words, picked_bytes[:, piece]), piece)
             y_banks.append(acc)
 
-        at_la, at_lb, smaller, larger, z_rows = {}, {}, {}, {}, {}
+        z_rows = {}
+        all_la = tile("at_la", [P, PACK * V], F32)
+        all_lb = tile("at_lb", [P, PACK * V], F32)
+        all_larger = tile("larger", [P, PACK * V], F32)
+        at_la = {t: all_la[:, cols(n, V)] for n, t in enumerate(PLANE_ORDER)}
+        at_lb = {t: all_lb[:, cols(n, V)] for n, t in enumerate(PLANE_ORDER)}
+        larger = {t: all_larger[:, cols(n, V)] for n, t in enumerate(PLANE_ORDER)}
+        smaller = {}
         pair_pieces = {t: (slice(0, V),) for t in PLANE_ORDER}
         pair_pieces[first] = (slice(0, V // 2), slice(V // 2, V))
         for t in PLANE_ORDER:
@@ -134,8 +141,6 @@ def tile_picked_sortlay_none_p_kernel(
             for (plane, piece), acc in zip(y_pieces, y_banks):
                 if plane == t:
                     scalar_copy(y_row[:, piece], acc[:])
-            at_la[t] = tile("at_la%d" % t, [P, V], F32)
-            at_lb[t] = tile("at_lb%d" % t, [P, V], F32)
             for piece in pair_pieces[t]:
                 copy = vector_copy if t == first and piece.start == 0 else scalar_copy
                 scalar_copy(at_la[t][:, piece], y_row[:].indirect(entries(la_list, piece)))
@@ -164,24 +169,27 @@ def tile_picked_sortlay_none_p_kernel(
         def take_smaller(t, piece):
             nc.vector.tensor_tensor(smaller[t][:, piece], at_la[t][:, piece], at_lb[t][:, piece], ALU.min)
 
-        def take_larger(t, tag):
-            larger[t] = tile("larger%d" % t, [P, V], F32, tag)
-            nc.vector.tensor_tensor(larger[t][:], at_la[t][:], at_lb[t][:], ALU.max)
+        def take_larger(stretch):
+            nc.vector.tensor_tensor(all_larger[:, stretch], all_la[:, stretch], all_lb[:, stretch], ALU.max)
+
+        cuts = (0, V // 2, V + V // 2, 2 * V + V // 2, PACK * V)
 
         def group_plane(t, copy_pairs):
             scalar_copy(z_grouped[0][:, :, t], z_rows[t][:, 0:QUARTER])
             copy_pairs(z_pairs[:, t // 2, :, t % 2], z_rows[t][:, QUARTER:S])
 
-        for t, following in zip(PLANE_ORDER, PLANE_ORDER[1:] + (None,)):
+        for n, (t, following) in enumerate(zip(PLANE_ORDER, PLANE_ORDER[1:] + (None,))):
             z_rows[t] = tile("z_row%d" % t, [P, S], F32, "z_row%d" % (first if t == last else t))
             for piece in pair_pieces[t]:
                 if t == first:
                     take_smaller(t, piece)
+                    if piece.start == 0:
+                        take_larger(slice(cuts[0], cuts[1]))
                 nc.vector.tensor_copy(z_rows[t][:].indirect(entries(la_list, piece)), smaller[t][:, piece])
-            take_larger(t, None if following is None else "y_row%d" % following)
             if following is not None:
+                take_larger(slice(cuts[n + 1], cuts[n + 2]))
                 take_smaller(following, slice(0, V))
-            nc.vector.tensor_copy(z_rows[t][:].indirect(lb_list[:]), larger[t][:])
+            nc.vector.tensor_copy(z_rows[t][:].indirect(lb_list[:]), larger[t])
             if t == PLANE_ORDER[2]:
                 w3_grouped.append(group_w3(0))
             if following is not None:
@@ -200,7 +208,7 @@ def tile_picked_sortlay_none_p_kernel(
 
         w2_mx = [quantize("w2_0", w2_grouped[0], "smaller%d" % last)]
         z_mx = [quantize_z(0)]
-        w2_mx.append(quantize("w2_1", w2_grouped[1], "larger%d" % last))
+        w2_mx.append(quantize("w2_1", w2_grouped[1], "larger"))
         z_mx.extend(quantize_z(q) for q in range(1, 4))
         w3_mx = [quantize("w3_0", w3_grouped[0], "z_row%d" % first)]
 
@@ -226,7 +234,7 @@ def tile_picked_sortlay_none_p_kernel(
         def fetch_mates(q):
             at_mate[q] = tile("at_mate%d" % q, [P, PACK, QUARTER], F32)
             for t in range(PACK):
-                copy = vector_copy if q == 0 and t >= 2 else scalar_copy
+                copy = vector_copy if q == 1 and t >= 1 else scalar_copy
                 copy(at_mate[q][:, t, :], h_rows[t][:].indirect(mate_list[:, cols(q, QUARTER // PER_COLUMN)]))
 
         def compete(q):

from contextlib import ExitStack

import concourse.mybir as mybir

K, T, S, V = 512, 2048, 512, 256
FLOPS = 3 * 2 * K * K * S

F32 = mybir.dt.float32
BF16 = mybir.dt.bfloat16
I32 = mybir.dt.int32
U32 = mybir.dt.uint32
U16 = mybir.dt.uint16
U8 = mybir.dt.uint8
FP8X4 = mybir.dt.float8_e4m3fn_x4
ALU = mybir.AluOpType
COPY = mybir.ActivationFunctionType.Copy

P = 128
PACK = 4
HALF = S // 2
QUARTER = S // 4
PER_COLUMN = 16
PLANE_ORDER = (2, 0, 1, 3)


def tile_picked_sortlay_none_p_kernel(
    tc, x_words, x_scales, w1, w2, res, w3, offs, la, lb, mate, out
):
    nc = tc.nc

    with ExitStack() as ctx:
        lists = ctx.enter_context(tc.tile_pool(name="lists", bufs=1))
        keep = ctx.enter_context(tc.tile_pool(name="keep", bufs=1))
        psum = ctx.enter_context(tc.psum_pool(name="psum", bufs=1))

        def tile(name, shape, dtype, tag=None):
            return keep.tile(shape, dtype, name=name, tag=tag or name, align_bytes=64)

        def bank(name, shape, number):
            return psum.tile(shape, F32, name=name, tag="bank%d" % number)

        def load_list(name, source):
            held = lists.tile(list(source.shape), U16, name=name)
            nc.sync.dma_start(held[:], source)
            return held

        def load_weight(name, source):
            raw = tile(name, [P, PACK, K], F32)
            nc.sync.dma_start(raw[:], source.rearrange("(p j) c -> p j c", j=PACK))
            return raw

        def scalar_copy(dst, src):
            nc.scalar.activation(dst, src, COPY)

        def vector_copy(dst, src):
            nc.vector.tensor_copy(dst, src)

        def deal_half(copy, name, raw, u):
            grouped = tile(name, [P, 2, P, PACK], BF16)
            copy(
                grouped[:].rearrange("p t m j -> p m j t"),
                raw[:].rearrange("p j (m t) -> p m j t", t=PACK)[:, :, :, 2 * u : 2 * u + 2],
            )
            return grouped[:].rearrange("p t m j -> p (t m j)")

        def quantize(name, grouped, tag=None):
            width = grouped.shape[1] // PACK
            codes = tile(name + "_codes", [P, width], U32, tag)
            scales = tile(name + "_scales", [P, width], U8)
            nc.vector.quantize_mx(out=codes[:].bitcast(FP8X4), scales=scales[:], in_=grouped)
            return codes, scales

        def product(acc, weights, weight_cols, tokens, token_cols):
            nc.tensor.matmul_mx(
                out=acc,
                lhsT=weights[0][:, weight_cols].bitcast(FP8X4),
                lhsT_scale=weights[1][:, weight_cols],
                rhs=tokens[0][:, token_cols].bitcast(FP8X4),
                rhs_scale=tokens[1],
                start=True,
                stop=True,
            )

        def cols(n, width):
            return slice(n * width, (n + 1) * width)

        def entries(held, piece):
            return held[:, piece.start // PER_COLUMN : piece.stop // PER_COLUMN]

        x_bytes = tile("x_bytes", [P, T], U8)
        nc.vector.memset(x_bytes[:].bitcast(I32), 0)
        offs_list = load_list("offs_list", offs)
        w1_raw = load_weight("w1_raw", w1)
        for quadrant in range(4):
            nc.sync.dma_start(
                x_bytes[32 * quadrant : 32 * quadrant + 4, :].bitcast(I32),
                x_scales[0, cols(quadrant, 4), :].bitcast(I32),
            )
        x_table = tile("x_table", [P, T], U32)
        nc.sync.dma_start(x_table[:].bitcast(I32), x_words[0].rearrange("p n t -> p (n t)").bitcast(I32))
        la_list = load_list("la_list", la)
        lb_list = load_list("lb_list", lb)
        w2_raw = load_weight("w2_raw", w2)
        w3_raw = load_weight("w3_raw", w3)
        mate_list = load_list("mate_list", mate)
        res_rows = []
        for q in range(4):
            rows = tile("res_rows%d" % q, [P, PACK, QUARTER], F32)
            nc.sync.dma_start(rows[:], res.rearrange("(m p) c -> p m c", p=P)[:, :, cols(q, QUARTER)])
            res_rows.append(rows)

        picked_bytes = tile("picked_bytes", [P, S], U8)
        nc.vector.tensor_copy(picked_bytes[:], x_bytes[:].indirect(offs_list[:]))
        w1_grouped = {1: deal_half(vector_copy, "w1_grouped1", w1_raw, 1), 0: deal_half(scalar_copy, "w1_grouped0", w1_raw, 0)}
        w1_mx = {u: quantize("w1_%d" % u, w1_grouped[u]) for u in (1, 0)}
        picked_words = tile("picked_words", [P, S], U32)
        token_pieces = (slice(0, HALF), slice(HALF, HALF + QUARTER), slice(HALF + QUARTER, S))
        for piece in token_pieces:
            nc.vector.tensor_copy(picked_words[:, piece], x_table[:].indirect(entries(offs_list, piece)))

        first, last = PLANE_ORDER[0], PLANE_ORDER[-1]
        y_pieces = [(first, piece) for piece in token_pieces] + [(t, slice(0, S)) for t in PLANE_ORDER[1:]]
        y_banks = []
        for number, (t, piece) in enumerate(y_pieces):
            acc = bank("y_bank%d" % number, [P, piece.stop - piece.start], min(number, 2))
            product(acc[:], w1_mx[t // 2], cols(t % 2, P), (picked_words, picked_bytes[:, piece]), piece)
            y_banks.append(acc)

        z_rows = {}
        all_la = tile("at_la", [P, PACK * V], F32)
        all_lb = tile("at_lb", [P, PACK * V], F32)
        all_larger = tile("larger", [P, PACK * V], F32)
        at_la = {t: all_la[:, cols(n, V)] for n, t in enumerate(PLANE_ORDER)}
        at_lb = {t: all_lb[:, cols(n, V)] for n, t in enumerate(PLANE_ORDER)}
        larger = {t: all_larger[:, cols(n, V)] for n, t in enumerate(PLANE_ORDER)}
        smaller = {}
        pair_pieces = {t: (slice(0, V),) for t in PLANE_ORDER}
        pair_pieces[first] = (slice(0, V // 2), slice(V // 2, V))
        for t in PLANE_ORDER:
            y_row = tile("y_row%d" % t, [P, S], F32)
            for (plane, piece), acc in zip(y_pieces, y_banks):
                if plane == t:
                    scalar_copy(y_row[:, piece], acc[:])
            for piece in pair_pieces[t]:
                copy = vector_copy if t == first and piece.start == 0 else scalar_copy
                scalar_copy(at_la[t][:, piece], y_row[:].indirect(entries(la_list, piece)))
                copy(at_lb[t][:, piece], y_row[:].indirect(entries(lb_list, piece)))

        w2_dealt = tile("w2_grouped", [P, PACK, P, PACK], BF16)
        scalar_copy(w2_dealt[:].rearrange("p t m j -> p m j t"), w2_raw[:].rearrange("p j (m t) -> p m j t", t=PACK))
        w2_grouped = [w2_dealt[:, 2 * u : 2 * u + 2].rearrange("p t m j -> p (t m j)") for u in range(2)]

        z_grouped = [tile("z_grouped%d" % q, [P, QUARTER, PACK], BF16) for q in range(4)]
        z_pairs = tile("z_pairs", [P, 2, S - QUARTER, 2], BF16)

        def group_w3(half):
            grouped = tile("w3_grouped%d" % half, [P, HALF, PACK], BF16)
            scalar_copy(
                grouped[:].rearrange("p (c i) j -> p c j i", i=4),
                w3_raw[:, :, cols(half, HALF)].rearrange("p j (c i) -> p c j i", i=4),
            )
            return grouped[:].rearrange("p c j -> p (c j)")

        w3_grouped = []

        for t in PLANE_ORDER:
            smaller[t] = tile("smaller%d" % t, [P, V], F32)

        def take_smaller(t, piece):
            nc.vector.tensor_tensor(smaller[t][:, piece], at_la[t][:, piece], at_lb[t][:, piece], ALU.min)

        def take_larger(stretch):
            nc.vector.tensor_tensor(all_larger[:, stretch], all_la[:, stretch], all_lb[:, stretch], ALU.max)

        cuts = (0, V // 2, V + V // 2, 2 * V + V // 2, PACK * V)

        def group_plane(t, copy_pairs):
            scalar_copy(z_grouped[0][:, :, t], z_rows[t][:, 0:QUARTER])
            copy_pairs(z_pairs[:, t // 2, :, t % 2], z_rows[t][:, QUARTER:S])

        for n, (t, following) in enumerate(zip(PLANE_ORDER, PLANE_ORDER[1:] + (None,))):
            z_rows[t] = tile("z_row%d" % t, [P, S], F32, "z_row%d" % (first if t == last else t))
            for piece in pair_pieces[t]:
                if t == first:
                    take_smaller(t, piece)
                    if piece.start == 0:
                        take_larger(slice(cuts[0], cuts[1]))
                nc.vector.tensor_copy(z_rows[t][:].indirect(entries(la_list, piece)), smaller[t][:, piece])
            if following is not None:
                take_larger(slice(cuts[n + 1], cuts[n + 2]))
                take_smaller(following, slice(0, V))
            nc.vector.tensor_copy(z_rows[t][:].indirect(lb_list[:]), larger[t])
            if t == PLANE_ORDER[2]:
                w3_grouped.append(group_w3(0))
            if following is not None:
                group_plane(t, scalar_copy)
        w3_grouped.append(group_w3(1))
        group_plane(last, vector_copy)
        pair_words = z_pairs[:].rearrange("p u c e -> p u (c e)").bitcast(F32)
        for q in range(1, 4):
            nc.scalar.copy(
                z_grouped[q][:].rearrange("p c t -> p (c t)").bitcast(F32).rearrange("p (c u) -> p c u", u=2),
                pair_words[:, :, cols(q - 1, QUARTER)].rearrange("p u c -> p c u"),
            )

        def quantize_z(q):
            return quantize("z_%d" % q, z_grouped[q][:].rearrange("p c t -> p (c t)"))

        w2_mx = [quantize("w2_0", w2_grouped[0], "smaller%d" % last)]
        z_mx = [quantize_z(0)]
        w2_mx.append(quantize("w2_1", w2_grouped[1], "larger"))
        z_mx.extend(quantize_z(q) for q in range(1, 4))
        w3_mx = [quantize("w3_0", w3_grouped[0], "z_row%d" % first)]

        h_tags = ("z_grouped3", "z_grouped2", "z_pairs", "z_grouped1")
        h_rows = [tile("h_row%d" % t, [P, S], F32, h_tags[t]) for t in range(PACK)]
        h_banks = []
        for q in range(4):
            acc = bank("h_bank%d" % q, [P, PACK, QUARTER], q)
            codes, scales = z_mx[q]
            for t in range(PACK):
                product(acc[:, t, :], w2_mx[t // 2], cols(t % 2, P), (codes, scales[:]), slice(0, QUARTER))
            h_banks.append(acc)
        for q in range(4):
            copy = vector_copy if q % 2 else scalar_copy
            for t in range(PACK):
                copy(h_rows[t][:, cols(q, QUARTER)], h_banks[q][:, t, :])
            if q == 1:
                w3_mx.append(quantize("w3_1", w3_grouped[1], "z_grouped0"))

        out_rows = out.rearrange("(m p) c -> p m c", p=P)
        at_mate, z2_grouped, out_banks = {}, {}, {}

        def fetch_mates(q):
            at_mate[q] = tile("at_mate%d" % q, [P, PACK, QUARTER], F32)
            for t in range(PACK):
                copy = vector_copy if q == 1 and t >= 1 else scalar_copy
                copy(at_mate[q][:, t, :], h_rows[t][:].indirect(mate_list[:, cols(q, QUARTER // PER_COLUMN)]))

        def compete(q):
            tag = ("z2_grouped0", "z2_grouped1", "z2_grouped0", "res_rows0")[q]
            z2_grouped[q] = tile("z2_grouped%d" % q, [P, QUARTER, PACK], BF16, tag)
            nc.vector.tensor_tensor(
                z2_grouped[q][:].rearrange("p (c i) t -> p c t i", i=4),
                h_banks[q][:].rearrange("p t (c i) -> p c t i", i=4),
                at_mate[q][:].rearrange("p t (c i) -> p c t i", i=4),
                ALU.max,
            )

        def last_product(q):
            codes, scales = quantize("z2_%d" % q, z2_grouped[q][:].rearrange("p c t -> p (c t)"))
            pieces = [(0, 2, 7), (2, 2, 0)] if q == 3 else [(0, 4, 4 + q)]
            out_banks[q] = []
            for first, count, number in pieces:
                acc = bank("out_bank%d_%d" % (q, first), [P, count, QUARTER], number)
                for m in range(first, first + count):
                    product(acc[:, m - first, :], w3_mx[m // 2], cols(m % 2, P), (codes, scales[:]), slice(0, QUARTER))
                out_banks[q].append((slice(first, first + count), acc))

        def finish(q):
            for blocks, acc in out_banks[q]:
                result = tile("result%d_%d" % (q, blocks.start), list(acc.shape), F32)
                nc.vector.tensor_tensor(result[:], acc[:], res_rows[q][:, blocks, :], ALU.add)
                nc.sync.dma_start(out_rows[:, blocks, cols(q, QUARTER)], result[:])

        for q in range(4):
            fetch_mates(q)
        compete(0)
        compete(1)
        last_product(0)
        last_product(1)
        compete(2)
        finish(0)
        last_product(2)
        compete(3)
        finish(1)
        last_product(3)
        finish(2)
        finish(3)
